import numpy as np
import ml_dtypes


def mxq(x, axis, fmt="e4m3"):
    dtype, down = {"e4m3": (ml_dtypes.float8_e4m3fn, 7), "e5m2": (ml_dtypes.float8_e5m2, 14)}[fmt]
    v = np.moveaxis(np.asarray(x, np.float32).astype(ml_dtypes.bfloat16).astype(np.float64), axis, -1)
    blocks = v.reshape(v.shape[:-1] + (-1, 32))
    amax = np.abs(blocks).max(-1, keepdims=True)
    byte = np.maximum(np.where(amax > 0, np.frexp(amax)[1] - 1 + 127, 0) - down, 1)
    scale = np.exp2(byte - 127.0)
    codes = (blocks / scale).astype(np.float32).astype(dtype).astype(np.float64)
    return np.moveaxis((codes * scale).reshape(v.shape), -1, axis)


WIDE = False


def mx_kscale(k):
    if not WIDE:
        return np.ones(k)
    levels = np.array([10, -10, 5, -5, 0])
    if k % 512:
        return np.exp2(np.random.permutation(np.resize(levels, k // 32))).repeat(32)
    a = np.empty((k // 512, 16))
    for p in range(k // 512):
        a[p, :8] = np.random.permutation(np.resize(levels, 8))
        for g in range(8):
            far = levels[np.abs(levels - a[p, g]) >= 10]
            a[p, g + 8] = far[np.random.randint(len(far))]
    return np.exp2(a.ravel()).repeat(32)


def f64(x):
    return np.asarray(x).astype(np.float64)


def striped(idx):
    return np.tile(idx.reshape(-1, 16).T, (8, 1)).astype(np.uint16)


def unstriped(offs):
    return offs[:16].T.reshape(-1).astype(np.int64)


E2M1 = np.array([0.0, 0.5, 1.0, 1.5, 2.0, 3.0, 4.0, 6.0, -0.0, -0.5, -1.0, -1.5, -2.0, -3.0, -4.0, -6.0])


def pack_weight(w, fmt):
    k, n = w.shape
    w = f64(np.asarray(w, np.float32).astype(ml_dtypes.bfloat16)).reshape(k // 32, 32, n)
    amax = np.abs(w).max(1)
    if fmt == "e4m3":
        byte = np.frexp(amax)[1] - 1 + 127 - 7
    else:
        mant, ex = np.frexp(amax / 6.0)
        byte = np.where(mant > 0.5, ex, ex - 1) + 127
    byte = np.clip(np.where(amax > 0, byte, 1), 1, 254)
    scaled = (w * np.exp2(127.0 - byte)[:, None, :]).reshape(k, n).astype(np.float32)
    by_word = np.ascontiguousarray(scaled.reshape(k // 512, 128, 4, n).transpose(0, 1, 3, 2))
    if fmt == "e4m3":
        words = by_word.astype(ml_dtypes.float8_e4m3fn).view(np.uint8)
    else:
        c = by_word.astype(ml_dtypes.float4_e2m1fn).view(np.uint8) & 0xF
        words = (c[..., 0::2] | (c[..., 1::2] << 4)).reshape(k // 512, 128, 2 * n)
    return np.ascontiguousarray(words), np.ascontiguousarray(byte.astype(np.uint8).reshape(k // 512, 16, n))


def unpack_weight(words, scales, fmt):
    g, _, n = scales.shape
    words = np.ascontiguousarray(words).reshape(g, 128, n, -1)
    if fmt == "e4m3":
        vals = words.view(ml_dtypes.float8_e4m3fn).astype(np.float64)
    else:
        nib = np.empty((g, 128, n, 4), np.uint8)
        nib[..., 0::2] = words & 0xF
        nib[..., 1::2] = words >> 4
        vals = E2M1[nib]
    vals = vals * np.repeat(np.exp2(scales.astype(np.float64) - 127.0), 8, axis=1)[..., None]
    return vals.transpose(0, 1, 3, 2).reshape(g * 512, n)


def gelu(v):
    return 0.5 * v * (1.0 + np.tanh(np.sqrt(2.0 / np.pi) * (v + 0.044715 * v**3)))


def bf(x):
    return np.asarray(x, np.float32).astype(ml_dtypes.bfloat16)


def planes(Y):
    n, m = Y.shape
    b = f64(bf(Y)).reshape(n // 32, 32, m)
    amax = np.abs(b).max(1)
    byte = np.clip(np.where(amax > 0, np.frexp(amax)[1] - 1 + 127 - 7, 1), 1, 254)
    codes = (b * np.exp2(127.0 - byte)[:, None, :]).reshape(n, m).astype(np.float32).astype(ml_dtypes.float8_e4m3fn).view(np.uint8)
    words = codes.reshape(n // 512, 128, 4, m).transpose(0, 1, 3, 2)
    return np.ascontiguousarray(words), np.ascontiguousarray(byte.astype(np.uint8).reshape(n // 512, 16, m))


K, H, N, T, S, T2, P = 1536, 512, 384, 2048, 1024, 2048, 512

def setup_inputs():
    n = np.random.standard_normal
    s = mx_kscale(K)[:, None]
    u = mx_kscale(H)[:, None]
    d = {}
    d["tab_words"], d["tab_scales"] = pack_weight(n((K, T)) * s, "e4m3")
    d["offs"] = striped(np.random.permutation(T)[:S])
    d["offs2"] = striped(np.random.permutation(T2)[:S])
    d["offs3"] = striped(np.random.permutation(T2)[:P])
    d["w1_words"], d["w1_scales"] = pack_weight(1.5 * n((K, H)) / K**0.5 / s, "e2m1")
    d["b1"] = (0.8 * n(H)).astype(np.float32)
    d["gain"] = (1.2 * np.exp(0.3 * n(H)) * u[:, 0]).astype(np.float32)
    d["w2"] = (n((K, H)) / K**0.5 / s * u.T).astype(np.float32)
    d["wgs"] = np.exp(0.3 * n((128, S))).astype(np.float32)
    d["page0"] = (n((H, T2)) * u).astype(np.float32)
    d["mu"] = (0.8 * n(H) * u[:, 0]).astype(np.float32)
    d["w3"] = (n((H, N)) / H**0.5 / u).astype(np.float32)
    return d

def reference(tab_words, tab_scales, offs, offs2, offs3, w1_words, w1_scales, b1, gain, w2, wgs, page0, mu, w3):
    v = unpack_weight(tab_words, tab_scales, "e4m3")[:, unstriped(offs)]
    w1 = unpack_weight(w1_words, w1_scales, "e2m1")
    bent = np.tanh((w1.T @ v) + f64(b1)[:, None])
    plain = mxq(f64(w2), 0, "e4m3").T @ v
    h = plain + f64(gain)[:, None] * bent
    page = f64(page0).copy()
    page[:, unstriped(offs2)] = np.tile(f64(wgs), (H // 128, 1)) * h
    x = np.abs(page[:, unstriped(offs3)] - f64(mu)[:, None])
    y = mxq(f64(w3), 0, "e4m3").T @ mxq(x, 0, "e4m3")
    words, scales = planes(page)
    return y, page, words, scales

@@ -1,0 +1,314 @@
+from contextlib import ExitStack
+
+import concourse.mybir as mybir
+
+K, H, N, T, S, T2, R = 1536, 512, 384, 2048, 1024, 2048, 512
+FLOPS = 2 * (2 * K * H * S + H * N * R)
+
+F32 = mybir.dt.float32
+BF16 = mybir.dt.bfloat16
+I32 = mybir.dt.int32
+U32 = mybir.dt.uint32
+U16 = mybir.dt.uint16
+U8 = mybir.dt.uint8
+FP8X4 = mybir.dt.float8_e4m3fn_x4
+FP4X4 = mybir.dt.float4_e2m1fn_x4
+ACT = mybir.ActivationFunctionType
+ALU = mybir.AluOpType
+
+P = 128
+PACK = 4
+PASSES = K // (P * PACK)
+QUADS = 4
+BANK = 512
+HALVES = S // BANK
+CHUNKS = T2 // BANK
+MOVED_ROWS = 112
+
+
+def tile_list_moromi_umami_features_kernel(
+    tc, tab_words, tab_scales, offs, offs2, offs3, w1_words, w1_scales, b1, gain, w2, wgs, page0, mu, w3,
+    out_0, out_1, out_2, out_3,
+):
+    nc = tc.nc
+    with ExitStack() as ctx:
+        lists = ctx.enter_context(tc.tile_pool(name="lists", bufs=1))
+        keep = ctx.enter_context(tc.tile_pool(name="keep", bufs=1))
+        ring = ctx.enter_context(tc.tile_pool(name="ring", bufs=2))
+        psum = ctx.enter_context(tc.psum_pool(name="psum", bufs=4))
+
+        idx = lists.tile([P, S // 16], U16, name="idx")
+        idx2 = lists.tile([P, S // 16], U16, name="idx2")
+        idx3 = lists.tile([P, R // 16], U16, name="idx3")
+
+        tab_sc = keep.tile([P, T], U8, name="tab_sc", align_bytes=64)
+        nc.vector.memset(tab_sc[:].bitcast(I32), 0)
+        w1_sc_raw = keep.tile([P, PASSES, H], U8, name="w1_sc_raw", align_bytes=64)
+        nc.vector.memset(w1_sc_raw[:].rearrange("p a c -> p (a c)").bitcast(I32), 0)
+        v_sc_moved = [keep.tile([P, S], U8, name="v_sc_moved%d" % a, align_bytes=64) for a in range(1, PASSES)]
+        for moved in v_sc_moved:
+            nc.vector.memset(moved[:].bitcast(I32), 0)
+        warm = keep.tile([P, 8], F32, name="warm")
+        nc.vector.memset(warm[:, 0:4], 0.0)
+        nc.scalar.activation(out=warm[:, 4:5], in_=warm[:, 0:1], func=ACT.Tanh)
+
+        nc.sync.dma_start(idx[:], offs)
+        for q in range(QUADS):
+            nc.gpsimd.dma_start(
+                out=tab_sc[32 * q : 32 * q + 4 * PASSES, :].bitcast(I32),
+                in_=tab_scales[:, 4 * q : 4 * q + 4, :].bitcast(I32),
+            )
+        for q in range(QUADS):
+            nc.scalar.dma_start(
+                out=w1_sc_raw[32 * q : 32 * q + 4, :, :].bitcast(I32),
+                in_=w1_scales[:, 4 * q : 4 * q + 4, :].rearrange("a r c -> r a c").bitcast(I32),
+            )
+        b1_sb = keep.tile([P, PACK], F32, name="b1_sb")
+        gain_sb = keep.tile([P, PACK], F32, name="gain_sb")
+        mu_sb = keep.tile([P, PACK], F32, name="mu_sb")
+
+        tab_w = [keep.tile([P, T], I32, name="tab_w%d" % a) for a in range(PASSES)]
+        w1_raw = keep.tile([P, PASSES, 2 * H], U8, name="w1_raw", align_bytes=64)
+        w2_raw = [keep.tile([P, PACK, H], F32, name="w2_raw%d" % a) for a in range(PASSES - 1)]
+        w2_last = [keep.tile([P, PACK, H // 2], F32, name="w2_last%d" % u) for u in range(2)]
+        w2_rows = w2.rearrange("(a p j) c -> a p j c", p=P, j=PACK)
+
+        def load_tab(a):
+            nc.sync.dma_start(out=tab_w[a][:], in_=tab_words[a].rearrange("p t i -> p (t i)").bitcast(I32))
+
+        nc.sync.dma_start(out=w1_raw[:].bitcast(I32), in_=w1_words.rearrange("a p c -> p a c").bitcast(I32))
+        load_tab(0)
+        nc.sync.dma_start(out=w2_raw[0][:], in_=w2_rows[0])
+        load_tab(1)
+        for sb, vec in ((b1_sb, b1), (gain_sb, gain)):
+            nc.sync.dma_start(out=sb[:], in_=vec.rearrange("(p t) -> p t", t=PACK))
+        nc.sync.dma_start(out=w2_raw[1][:], in_=w2_rows[1])
+        load_tab(2)
+        for u in range(2):
+            nc.sync.dma_start(out=w2_last[u][:], in_=w2_rows[2][:, :, u * (H // 2) : (u + 1) * (H // 2)])
+
+        wgs_rows = wgs.rearrange("(i t) s -> i t s", t=PACK)
+        wgs_sb = [keep.tile([P, S], F32, name="wgs_sb%d" % t) for t in range(PACK)]
+        pages = [keep.tile([P, T2], F32, name="page%d" % t) for t in range(PACK)]
+        page_rows = page0.rearrange("(p t) m -> p t m", t=PACK)
+        out_1_rows = out_1.rearrange("(p t) m -> p t m", t=PACK)
+
+        def load_wgs(t, queue):
+            for q in (0, 2, 1, 3):
+                queue.dma_start(out=wgs_sb[t][32 * q : 32 * q + 32, :], in_=wgs_rows[:, t, :])
+
+        load_wgs(0, nc.scalar)
+        nc.sync.dma_start(idx2[:], offs2)
+        nc.sync.dma_start(out=pages[0][:], in_=page_rows[:, 0, :])
+        nc.sync.dma_start(idx3[:], offs3)
+        nc.sync.dma_start(out=mu_sb[:], in_=mu.rearrange("(p t) -> p t", t=PACK))
+        w3_raw = keep.tile([P, PACK, N], F32, name="w3_raw")
+        for t in range(1, PACK):
+            load_wgs(t, nc.sync)
+            nc.sync.dma_start(out=pages[t][:], in_=page_rows[:, t, :])
+            if t == 1:
+                nc.sync.dma_start(out=w3_raw[:], in_=w3.rearrange("(p j) n -> p j n", j=PACK))
+
+        v_sc = keep.tile([P, S], U8, name="v_sc", align_bytes=64)
+        nc.vector.tensor_copy(out=v_sc[:], in_=tab_sc[:].indirect(idx[:]))
+        for a in range(1, PASSES):
+            nc.scalar.dma_start(
+                out=v_sc_moved[a - 1][0:MOVED_ROWS, :].bitcast(I32),
+                in_=v_sc[4 * a : 4 * a + MOVED_ROWS, :].bitcast(I32),
+            )
+        v_sc_zero = [v_sc] + v_sc_moved
+
+        v_w = [[None] * HALVES for a in range(PASSES)]
+
+        def gather_words(a, whole):
+            if whole:
+                both = keep.tile([P, S], U32, name="v_w%d" % a, align_bytes=64)
+                nc.vector.tensor_copy(out=both[:], in_=tab_w[a][:].bitcast(U32).indirect(idx[:]))
+                for u in range(HALVES):
+                    v_w[a][u] = both[:, u * BANK : (u + 1) * BANK]
+            else:
+                for u in range(HALVES):
+                    half = keep.tile([P, BANK], U32, name="v_w%d_%d" % (a, u), align_bytes=64)
+                    nc.vector.tensor_copy(
+                        out=half[:],
+                        in_=tab_w[a][:].bitcast(U32).indirect(idx[:, u * (BANK // 16) : (u + 1) * (BANK // 16)]),
+                    )
+                    v_w[a][u] = half[:]
+
+        w2_bf = [keep.tile([P, PACK, P, PACK], BF16, name="w2_bf%d" % a, align_bytes=64) for a in range(PASSES)]
+        w2_codes = [keep.tile([P, H], U32, name="w2_codes%d" % a, align_bytes=64) for a in range(PASSES)]
+        w2_sc = [keep.tile([P, H], U8, name="w2_sc%d" % a, align_bytes=64) for a in range(PASSES)]
+
+        def deal_w2(engine_copy, a, raw, m0, m1):
+            engine_copy(
+                out=w2_bf[a][:, :, m0:m1, :].rearrange("p t m j -> p m j t"),
+                in_=raw[:].rearrange("p j (m t) -> p m j t", t=PACK),
+            )
+
+        def quantize_w2(a, t0, t1):
+            nc.vector.quantize_mx(
+                out=w2_codes[a][:, t0 * P : t1 * P].bitcast(FP8X4),
+                scales=w2_sc[a][:, t0 * P : t1 * P],
+                in_=w2_bf[a][:, t0:t1, :, :].rearrange("p t m j -> p (t m j)"),
+            )
+
+        w1_codes = keep.tile([P, PASSES, PACK, 2 * P], U8, name="w1_codes", align_bytes=64)
+        w1_sc = keep.tile([P, PASSES, PACK, P], U8, name="w1_sc", align_bytes=64)
+        nc.vector.tensor_copy(
+            out=w1_codes[:].bitcast(U16).rearrange("p a t m -> p a m t"),
+            in_=w1_raw[:].bitcast(U16).rearrange("p a (m t) -> p a m t", t=PACK),
+        )
+        gather_words(0, True)
+        nc.vector.tensor_copy(
+            out=w1_sc[:],
+            in_=w1_sc_raw[:].rearrange("p a (m t) -> p a t m", t=PACK),
+        )
+        deal_w2(nc.scalar.copy, 0, w2_raw[0], 0, P)
+        gather_words(1, True)
+        quantize_w2(0, 0, PACK)
+        deal_w2(nc.scalar.copy, 1, w2_raw[1], 0, P)
+        gather_words(2, False)
+        quantize_w2(1, 0, PACK)
+        deal_w2(nc.scalar.copy, 2, w2_last[0], 0, P // 2)
+        deal_w2(nc.vector.tensor_copy, 2, w2_last[1], P // 2, P)
+        quantize_w2(2, 0, 1)
+        quantize_w2(2, 1, 2)
+        quantize_w2(2, 2, 4)
+
+        w3_bf = keep.tile([P, N, PACK], BF16, name="w3_bf", align_bytes=64)
+        w3_codes = keep.tile([P, N], U32, name="w3_codes", align_bytes=64)
+        w3_sc = keep.tile([P, N], U8, name="w3_sc", align_bytes=64)
+
+        def prepare_w3():
+            nc.scalar.copy(
+                out=w3_bf[:].rearrange("p (c i) j -> p c j i", i=4),
+                in_=w3_raw[:].rearrange("p j (c i) -> p c j i", i=4),
+            )
+            for n0, n1 in ((0, 256), (256, N)):
+                nc.vector.quantize_mx(
+                    out=w3_codes[:, n0:n1].bitcast(FP8X4),
+                    scales=w3_sc[:, n0:n1],
+                    in_=w3_bf[:, n0:n1, :].rearrange("p n j -> p (n j)"),
+                )
+
+        h = [keep.tile([P, S], F32, name="h%d" % t) for t in range(PACK)]
+        x_bf = keep.tile([P, R, PACK], BF16, name="x_bf", align_bytes=64)
+        page_bf = [keep.tile([P, BANK, PACK], BF16, name="page_bf%d" % c, align_bytes=64) for c in range(CHUNKS)]
+
+        def make_h(t):
+            for u in range(HALVES):
+                cols = slice(u * BANK, (u + 1) * BANK)
+                z = psum.tile([P, BANK], F32, name="z")
+                for a in range(PASSES):
+                    nc.tensor.matmul_mx(
+                        out=z[:],
+                        lhsT=w1_codes[:, a, t, :].bitcast(FP4X4),
+                        lhsT_scale=w1_sc[:, a, t, :],
+                        rhs=v_w[a][u].bitcast(FP8X4),
+                        rhs_scale=v_sc_zero[a][:, cols],
+                        start=(a == 0),
+                        stop=(a == PASSES - 1),
+                    )
+                plain = psum.tile([P, BANK], F32, name="plain")
+                for a in range(PASSES):
+                    nc.tensor.matmul_mx(
+                        out=plain[:],
+                        lhsT=w2_codes[a][:, t * P : (t + 1) * P].bitcast(FP8X4),
+                        lhsT_scale=w2_sc[a][:, t * P : (t + 1) * P],
+                        rhs=v_w[a][u].bitcast(FP8X4),
+                        rhs_scale=v_sc[4 * a : P, cols],
+                        start=(a == 0),
+                        stop=(a == PASSES - 1),
+                    )
+                nc.scalar.activation(out=h[t][:, cols], in_=z[:], func=ACT.Tanh, bias=b1_sb[:, t : t + 1])
+                nc.vector.scalar_tensor_tensor(
+                    out=h[t][:, cols],
+                    in0=h[t][:, cols],
+                    scalar=gain_sb[:, t : t + 1],
+                    in1=plain[:],
+                    op0=ALU.mult,
+                    op1=ALU.add,
+                )
+                if t == 0:
+                    nc.vector.tensor_tensor(
+                        pages[t][:].indirect(idx2[:, u * (BANK // 16) : (u + 1) * (BANK // 16)]),
+                        h[t][:, cols],
+                        wgs_sb[t][:, cols],
+                        ALU.mult,
+                    )
+
+        def round_page(engine_copy, t, c):
+            cols = pages[t][:, c * BANK : (c + 1) * BANK]
+            if t == PACK - 2 and c in (1, 2):
+                engine_copy(out=page_bf[c][:, :, t : t + 2], in_=cols.unsqueeze(2).to_broadcast([P, BANK, 2]))
+            else:
+                engine_copy(out=page_bf[c][:, :, t], in_=cols)
+
+        def pick_x(t):
+            picked = ring.tile([P, R], F32, name="picked")
+            nc.vector.tensor_copy(out=picked[:], in_=pages[t][:].indirect(idx3[:]))
+            nc.scalar.activation(out=x_bf[:, :, t], in_=picked[:], func=ACT.Abs, bias=mu_sb[:, t : t + 1], scale=-1.0)
+
+        make_h(0)
+        for t in range(PACK):
+            if t > 0:
+                nc.vector.tensor_tensor(pages[t][:].indirect(idx2[:]), h[t][:], wgs_sb[t][:], ALU.mult)
+            store_queue = nc.gpsimd if t + 1 < PACK else nc.sync
+            store_queue.dma_start(out=out_1_rows[:, t, :], in_=pages[t][:])
+            if t + 1 < PACK:
+                make_h(t + 1)
+                if t == 0:
+                    prepare_w3()
+                pick_x(t)
+                for c in range(CHUNKS):
+                    round_page(nc.scalar.copy, t, c)
+
+        last = PACK - 1
+        y_codes = [keep.tile([P, BANK], U32, name="y_codes%d" % c, align_bytes=64) for c in range(CHUNKS)]
+        y_sc = keep.tile([P, T2], U8, name="y_sc", align_bytes=64)
+        out_2_words = out_2[0].rearrange("p m i -> p (m i)").bitcast(I32)
+
+        def quantize_page(c):
+            nc.vector.quantize_mx(
+                out=y_codes[c][:].bitcast(FP8X4),
+                scales=y_sc[:, c * BANK : (c + 1) * BANK],
+                in_=page_bf[c][:].rearrange("p m t -> p (m t)"),
+            )
+            nc.sync.dma_start(out=out_2_words[:, c * BANK : (c + 1) * BANK], in_=y_codes[c][:].bitcast(I32))
+
+        round_page(nc.scalar.copy, last, 0)
+        pick_x(last)
+        round_page(nc.vector.tensor_copy, last, 1)
+        quantize_page(0)
+        round_page(nc.vector.tensor_copy, last, 2)
+        round_page(nc.scalar.copy, last, 3)
+
+        x_codes = keep.tile([P, R], U32, name="x_codes", align_bytes=64)
+        x_sc = keep.tile([P, R], U8, name="x_sc", align_bytes=64)
+        nc.vector.quantize_mx(
+            out=x_codes[:].bitcast(FP8X4), scales=x_sc[:], in_=x_bf[:].rearrange("p m t -> p (m t)")
+        )
+        for c in range(1, CHUNKS):
+            quantize_page(c)
+        for q in range(QUADS):
+            nc.sync.dma_start(
+                out=out_3[0, 4 * q : 4 * q + 4, :].bitcast(I32), in_=y_sc[32 * q : 32 * q + 4, :].bitcast(I32)
+            )
+
+        for b in range(N // P):
+            acc = psum.tile([P, R], F32, name="z")
+            nc.tensor.matmul_mx(
+                out=acc[:],
+                lhsT=w3_codes[:, b * P : (b + 1) * P].bitcast(FP8X4),
+                lhsT_scale=w3_sc[:, b * P : (b + 1) * P],
+                rhs=x_codes[:].bitcast(FP8X4),
+                rhs_scale=x_sc[:],
+                start=True,
+                stop=True,
+            )
+            y = keep.tile([P, R], F32, name="y%d" % b)
+            if b == 1:
+                nc.vector.tensor_copy(out=y[:], in_=acc[:])
+            else:
+                nc.scalar.copy(out=y[:], in_=acc[:])
+            nc.sync.dma_start(out=out_0[b * P : (b + 1) * P, :], in_=y[:])

@@ -53,16 +53,6 @@ def tile_list_moromi_umami_features_kernel(
         nc.scalar.activation(out=warm[:, 4:5], in_=warm[:, 0:1], func=ACT.Tanh)
 
         nc.sync.dma_start(idx[:], offs)
-        for q in range(QUADS):
-            nc.gpsimd.dma_start(
-                out=tab_sc[32 * q : 32 * q + 4 * PASSES, :].bitcast(I32),
-                in_=tab_scales[:, 4 * q : 4 * q + 4, :].bitcast(I32),
-            )
-        for q in range(QUADS):
-            nc.scalar.dma_start(
-                out=w1_sc_raw[32 * q : 32 * q + 4, :, :].bitcast(I32),
-                in_=w1_scales[:, 4 * q : 4 * q + 4, :].rearrange("a r c -> r a c").bitcast(I32),
-            )
         b1_sb = keep.tile([P, PACK], F32, name="b1_sb")
         gain_sb = keep.tile([P, PACK], F32, name="gain_sb")
         mu_sb = keep.tile([P, PACK], F32, name="mu_sb")
@@ -76,9 +66,19 @@ def tile_list_moromi_umami_features_kernel(
         def load_tab(a):
             nc.sync.dma_start(out=tab_w[a][:], in_=tab_words[a].rearrange("p t i -> p (t i)").bitcast(I32))
 
-        nc.sync.dma_start(out=w1_raw[:].bitcast(I32), in_=w1_words.rearrange("a p c -> p a c").bitcast(I32))
         load_tab(0)
+        for q in range(QUADS):
+            nc.sync.dma_start(
+                out=tab_sc[32 * q : 32 * q + 4 * PASSES, :].bitcast(I32),
+                in_=tab_scales[:, 4 * q : 4 * q + 4, :].bitcast(I32),
+            )
+        nc.sync.dma_start(out=w1_raw[:].bitcast(I32), in_=w1_words.rearrange("a p c -> p a c").bitcast(I32))
         nc.sync.dma_start(out=w2_raw[0][:], in_=w2_rows[0])
+        for q in range(QUADS):
+            nc.sync.dma_start(
+                out=w1_sc_raw[32 * q : 32 * q + 4, :, :].bitcast(I32),
+                in_=w1_scales[:, 4 * q : 4 * q + 4, :].rearrange("a r c -> r a c").bitcast(I32),
+            )
         load_tab(1)
         for sb, vec in ((b1_sb, b1), (gain_sb, gain)):
             nc.sync.dma_start(out=sb[:], in_=vec.rearrange("(p t) -> p t", t=PACK))
@@ -97,22 +97,21 @@ def tile_list_moromi_umami_features_kernel(
             for q in (0, 2, 1, 3):
                 queue.dma_start(out=wgs_sb[t][32 * q : 32 * q + 32, :], in_=wgs_rows[:, t, :])
 
-        load_wgs(0, nc.scalar)
         nc.sync.dma_start(idx2[:], offs2)
+        load_wgs(0, nc.sync)
         nc.sync.dma_start(out=pages[0][:], in_=page_rows[:, 0, :])
         nc.sync.dma_start(idx3[:], offs3)
         nc.sync.dma_start(out=mu_sb[:], in_=mu.rearrange("(p t) -> p t", t=PACK))
         w3_raw = keep.tile([P, PACK, N], F32, name="w3_raw")
+        nc.sync.dma_start(out=w3_raw[:], in_=w3.rearrange("(p j) n -> p j n", j=PACK))
         for t in range(1, PACK):
             load_wgs(t, nc.sync)
             nc.sync.dma_start(out=pages[t][:], in_=page_rows[:, t, :])
-            if t == 1:
-                nc.sync.dma_start(out=w3_raw[:], in_=w3.rearrange("(p j) n -> p j n", j=PACK))
 
         v_sc = keep.tile([P, S], U8, name="v_sc", align_bytes=64)
         nc.vector.tensor_copy(out=v_sc[:], in_=tab_sc[:].indirect(idx[:]))
         for a in range(1, PASSES):
-            nc.scalar.dma_start(
+            nc.gpsimd.dma_start(
                 out=v_sc_moved[a - 1][0:MOVED_ROWS, :].bitcast(I32),
                 in_=v_sc[4 * a : 4 * a + MOVED_ROWS, :].bitcast(I32),
             )
@@ -141,8 +140,8 @@ def tile_list_moromi_umami_features_kernel(
 
         def deal_w2(engine_copy, a, raw, m0, m1):
             engine_copy(
-                out=w2_bf[a][:, :, m0:m1, :].rearrange("p t m j -> p m j t"),
-                in_=raw[:].rearrange("p j (m t) -> p m j t", t=PACK),
+                out=w2_bf[a][:, :, m0:m1, :].rearrange("p t m j -> p m t j"),
+                in_=raw[:].rearrange("p j (m t) -> p m t j", t=PACK),
             )
 
         def quantize_w2(a, t0, t1):
@@ -152,11 +151,11 @@ def tile_list_moromi_umami_features_kernel(
                 in_=w2_bf[a][:, t0:t1, :, :].rearrange("p t m j -> p (t m j)"),
             )
 
-        w1_codes = keep.tile([P, PASSES, PACK, 2 * P], U8, name="w1_codes", align_bytes=64)
-        w1_sc = keep.tile([P, PASSES, PACK, P], U8, name="w1_sc", align_bytes=64)
+        w1_codes = keep.tile([P, PASSES, PACK, 2 * P], U8, name="w1_codes", tag="after_z_a", align_bytes=64)
+        w1_sc = keep.tile([P, PASSES, PACK, P], U8, name="w1_sc", tag="after_z_b", align_bytes=64)
         nc.vector.tensor_copy(
-            out=w1_codes[:].bitcast(U16).rearrange("p a t m -> p a m t"),
-            in_=w1_raw[:].bitcast(U16).rearrange("p a (m t) -> p a m t", t=PACK),
+            out=w1_codes[:].bitcast(U16),
+            in_=w1_raw[:].bitcast(U16).rearrange("p a (m t) -> p a t m", t=PACK),
         )
         gather_words(0, True)
         nc.vector.tensor_copy(
@@ -191,51 +190,70 @@ def tile_list_moromi_umami_features_kernel(
                     in_=w3_bf[:, n0:n1, :].rearrange("p n j -> p (n j)"),
                 )
 
-        h = [keep.tile([P, S], F32, name="h%d" % t) for t in range(PACK)]
-        x_bf = keep.tile([P, R, PACK], BF16, name="x_bf", align_bytes=64)
-        page_bf = [keep.tile([P, BANK, PACK], BF16, name="page_bf%d" % c, align_bytes=64) for c in range(CHUNKS)]
+        bent = [keep.tile([P, S], F32, name="bent%d" % t) for t in range(PACK)]
+        h = {}
 
-        def make_h(t):
-            for u in range(HALVES):
-                cols = slice(u * BANK, (u + 1) * BANK)
-                z = psum.tile([P, BANK], F32, name="z")
-                for a in range(PASSES):
-                    nc.tensor.matmul_mx(
-                        out=z[:],
-                        lhsT=w1_codes[:, a, t, :].bitcast(FP4X4),
-                        lhsT_scale=w1_sc[:, a, t, :],
-                        rhs=v_w[a][u].bitcast(FP8X4),
-                        rhs_scale=v_sc_zero[a][:, cols],
-                        start=(a == 0),
-                        stop=(a == PASSES - 1),
-                    )
-                plain = psum.tile([P, BANK], F32, name="plain")
-                for a in range(PASSES):
-                    nc.tensor.matmul_mx(
-                        out=plain[:],
-                        lhsT=w2_codes[a][:, t * P : (t + 1) * P].bitcast(FP8X4),
-                        lhsT_scale=w2_sc[a][:, t * P : (t + 1) * P],
-                        rhs=v_w[a][u].bitcast(FP8X4),
-                        rhs_scale=v_sc[4 * a : P, cols],
-                        start=(a == 0),
-                        stop=(a == PASSES - 1),
-                    )
-                nc.scalar.activation(out=h[t][:, cols], in_=z[:], func=ACT.Tanh, bias=b1_sb[:, t : t + 1])
-                nc.vector.scalar_tensor_tensor(
-                    out=h[t][:, cols],
-                    in0=h[t][:, cols],
-                    scalar=gain_sb[:, t : t + 1],
-                    in1=plain[:],
-                    op0=ALU.mult,
-                    op1=ALU.add,
+        def bend(t, u):
+            cols = slice(u * BANK, (u + 1) * BANK)
+            z = psum.tile([P, BANK], F32, name="z")
+            for a in range(PASSES):
+                nc.tensor.matmul_mx(
+                    out=z[:],
+                    lhsT=w1_codes[:, a, t, :].bitcast(FP4X4),
+                    lhsT_scale=w1_sc[:, a, t, :],
+                    rhs=v_w[a][u].bitcast(FP8X4),
+                    rhs_scale=v_sc_zero[a][:, cols],
+                    start=(a == 0),
+                    stop=(a == PASSES - 1),
                 )
-                if t == 0:
-                    nc.vector.tensor_tensor(
-                        pages[t][:].indirect(idx2[:, u * (BANK // 16) : (u + 1) * (BANK // 16)]),
-                        h[t][:, cols],
-                        wgs_sb[t][:, cols],
-                        ALU.mult,
-                    )
+            nc.scalar.activation(out=bent[t][:, cols], in_=z[:], func=ACT.Tanh, bias=b1_sb[:, t : t + 1])
+
+        def add_plain(t, u):
+            cols = slice(u * BANK, (u + 1) * BANK)
+            if u == 0:
+                h[t] = ring.tile([P, S], F32, name="h")
+            plain = psum.tile([P, BANK], F32, name="plain")
+            for a in range(PASSES):
+                nc.tensor.matmul_mx(
+                    out=plain[:],
+                    lhsT=w2_codes[a][:, t * P : (t + 1) * P].bitcast(FP8X4),
+                    lhsT_scale=w2_sc[a][:, t * P : (t + 1) * P],
+                    rhs=v_w[a][u].bitcast(FP8X4),
+                    rhs_scale=v_sc[4 * a : P, cols],
+                    start=(a == 0),
+                    stop=(a == PASSES - 1),
+                )
+            nc.vector.scalar_tensor_tensor(
+                out=h[t][:, cols],
+                in0=bent[t][:, cols],
+                scalar=gain_sb[:, t : t + 1],
+                in1=plain[:],
+                op0=ALU.mult,
+                op1=ALU.add,
+            )
+
+        for u in range(HALVES):
+            cols = slice(u * BANK, (u + 1) * BANK)
+            bend(0, u)
+            add_plain(0, u)
+            nc.vector.tensor_tensor(
+                pages[0][:].indirect(idx2[:, u * (BANK // 16) : (u + 1) * (BANK // 16)]),
+                h[0][:, cols],
+                wgs_sb[0][:, cols],
+                ALU.mult,
+            )
+        for u in range(HALVES):
+            bend(1, u)
+        for u in range(HALVES):
+            add_plain(1, u)
+        for t in range(2, PACK):
+            for u in range(HALVES):
+                bend(t, u)
+        prepare_w3()
+
+        x_bf = keep.tile([P, R, PACK], BF16, name="x_bf", tag="after_z_b", align_bytes=64)
+        page_all = keep.tile([P, T2, PACK], BF16, name="page_bf", tag="after_z_a", align_bytes=64)
+        page_bf = [page_all[:, c * BANK : (c + 1) * BANK, :] for c in range(CHUNKS)]
 
         def round_page(engine_copy, t, c):
             cols = pages[t][:, c * BANK : (c + 1) * BANK]
@@ -245,20 +263,19 @@ def tile_list_moromi_umami_features_kernel(
                 engine_copy(out=page_bf[c][:, :, t], in_=cols)
 
         def pick_x(t):
-            picked = ring.tile([P, R], F32, name="picked")
+            picked = keep.tile([P, R], F32, name="picked%d" % t)
             nc.vector.tensor_copy(out=picked[:], in_=pages[t][:].indirect(idx3[:]))
             nc.scalar.activation(out=x_bf[:, :, t], in_=picked[:], func=ACT.Abs, bias=mu_sb[:, t : t + 1], scale=-1.0)
 
-        make_h(0)
         for t in range(PACK):
             if t > 0:
                 nc.vector.tensor_tensor(pages[t][:].indirect(idx2[:]), h[t][:], wgs_sb[t][:], ALU.mult)
             store_queue = nc.gpsimd if t + 1 < PACK else nc.sync
             store_queue.dma_start(out=out_1_rows[:, t, :], in_=pages[t][:])
             if t + 1 < PACK:
-                make_h(t + 1)
-                if t == 0:
-                    prepare_w3()
+                if t > 0:
+                    for u in range(HALVES):
+                        add_plain(t + 1, u)
                 pick_x(t)
                 for c in range(CHUNKS):
                     round_page(nc.scalar.copy, t, c)
@@ -272,7 +289,7 @@ def tile_list_moromi_umami_features_kernel(
             nc.vector.quantize_mx(
                 out=y_codes[c][:].bitcast(FP8X4),
                 scales=y_sc[:, c * BANK : (c + 1) * BANK],
-                in_=page_bf[c][:].rearrange("p m t -> p (m t)"),
+                in_=page_bf[c].rearrange("p m t -> p (m t)"),
             )
             nc.sync.dma_start(out=out_2_words[:, c * BANK : (c + 1) * BANK], in_=y_codes[c][:].bitcast(I32))
 

@@ -35,6 +35,7 @@ def tile_list_moromi_umami_features_kernel(
         lists = ctx.enter_context(tc.tile_pool(name="lists", bufs=1))
         keep = ctx.enter_context(tc.tile_pool(name="keep", bufs=1))
         ring = ctx.enter_context(tc.tile_pool(name="ring", bufs=2))
+        reuse = ctx.enter_context(tc.tile_pool(name="reuse", bufs=1))
         psum = ctx.enter_context(tc.psum_pool(name="psum", bufs=4))
 
         idx = lists.tile([P, S // 16], U16, name="idx")
@@ -58,60 +59,52 @@ def tile_list_moromi_umami_features_kernel(
         mu_sb = keep.tile([P, PACK], F32, name="mu_sb")
 
         tab_w = [keep.tile([P, T], I32, name="tab_w%d" % a) for a in range(PASSES)]
-        w1_raw = keep.tile([P, PASSES, 2 * H], U8, name="w1_raw", align_bytes=64)
+        w1_raw = keep.tile([P, PASSES, 2 * H], U8, name="w1_raw")
         w2_raw = [keep.tile([P, PACK, H], F32, name="w2_raw%d" % a) for a in range(PASSES - 1)]
         w2_last = [keep.tile([P, PACK, H // 2], F32, name="w2_last%d" % u) for u in range(2)]
         w2_rows = w2.rearrange("(a p j) c -> a p j c", p=P, j=PACK)
+        wgs_rows = wgs.rearrange("(i t) s -> i t s", t=PACK)
+        page_rows = page0.rearrange("(p t) m -> p t m", t=PACK)
+        out_1_rows = out_1.rearrange("(p t) m -> p t m", t=PACK)
 
         def load_tab(a):
             nc.sync.dma_start(out=tab_w[a][:], in_=tab_words[a].rearrange("p t i -> p (t i)").bitcast(I32))
 
-        load_tab(0)
+        def load_wgs(tile, t0, t1, q):
+            nc.sync.dma_start(out=tile[32 * q : 32 * q + 32, :, :], in_=wgs_rows[:, t0:t1, :])
+
+        for sb, vec in ((b1_sb, b1), (gain_sb, gain)):
+            nc.scalar.dma_start(out=sb[:], in_=vec.rearrange("(p t) -> p t", t=PACK))
         for q in range(QUADS):
-            nc.sync.dma_start(
+            nc.scalar.dma_start(
                 out=tab_sc[32 * q : 32 * q + 4 * PASSES, :].bitcast(I32),
                 in_=tab_scales[:, 4 * q : 4 * q + 4, :].bitcast(I32),
             )
-        nc.sync.dma_start(out=w1_raw[:].bitcast(I32), in_=w1_words.rearrange("a p c -> p a c").bitcast(I32))
-        nc.sync.dma_start(out=w2_raw[0][:], in_=w2_rows[0])
         for q in range(QUADS):
-            nc.sync.dma_start(
+            nc.scalar.dma_start(
                 out=w1_sc_raw[32 * q : 32 * q + 4, :, :].bitcast(I32),
                 in_=w1_scales[:, 4 * q : 4 * q + 4, :].rearrange("a r c -> r a c").bitcast(I32),
             )
+
+        wgs_first = keep.tile([P, 1, S], F32, name="wgs_first")
+        load_tab(0)
+        nc.sync.dma_start(out=w1_raw[:].bitcast(I32), in_=w1_words.rearrange("a p c -> p a c").bitcast(I32))
+        nc.sync.dma_start(out=w2_raw[0][:], in_=w2_rows[0])
+        load_wgs(wgs_first, 0, 1, 0)
         load_tab(1)
-        for sb, vec in ((b1_sb, b1), (gain_sb, gain)):
-            nc.sync.dma_start(out=sb[:], in_=vec.rearrange("(p t) -> p t", t=PACK))
+        load_wgs(wgs_first, 0, 1, 2)
         nc.sync.dma_start(out=w2_raw[1][:], in_=w2_rows[1])
+        load_wgs(wgs_first, 0, 1, 1)
         load_tab(2)
+        load_wgs(wgs_first, 0, 1, 3)
         for u in range(2):
             nc.sync.dma_start(out=w2_last[u][:], in_=w2_rows[2][:, :, u * (H // 2) : (u + 1) * (H // 2)])
-
-        wgs_rows = wgs.rearrange("(i t) s -> i t s", t=PACK)
-        wgs_sb = [keep.tile([P, S], F32, name="wgs_sb%d" % t) for t in range(PACK)]
-        pages = [keep.tile([P, T2], F32, name="page%d" % t) for t in range(PACK)]
-        page_rows = page0.rearrange("(p t) m -> p t m", t=PACK)
-        out_1_rows = out_1.rearrange("(p t) m -> p t m", t=PACK)
-
-        def load_wgs(t, queue):
-            for q in (0, 2, 1, 3):
-                queue.dma_start(out=wgs_sb[t][32 * q : 32 * q + 32, :], in_=wgs_rows[:, t, :])
-
         nc.sync.dma_start(idx2[:], offs2)
-        load_wgs(0, nc.sync)
-        nc.sync.dma_start(out=pages[0][:], in_=page_rows[:, 0, :])
-        nc.sync.dma_start(idx3[:], offs3)
-        nc.sync.dma_start(out=mu_sb[:], in_=mu.rearrange("(p t) -> p t", t=PACK))
-        w3_raw = keep.tile([P, PACK, N], F32, name="w3_raw")
-        nc.sync.dma_start(out=w3_raw[:], in_=w3.rearrange("(p j) n -> p j n", j=PACK))
-        for t in range(1, PACK):
-            load_wgs(t, nc.sync)
-            nc.sync.dma_start(out=pages[t][:], in_=page_rows[:, t, :])
 
         v_sc = keep.tile([P, S], U8, name="v_sc", align_bytes=64)
         nc.vector.tensor_copy(out=v_sc[:], in_=tab_sc[:].indirect(idx[:]))
         for a in range(1, PASSES):
-            nc.gpsimd.dma_start(
+            nc.scalar.dma_start(
                 out=v_sc_moved[a - 1][0:MOVED_ROWS, :].bitcast(I32),
                 in_=v_sc[4 * a : 4 * a + MOVED_ROWS, :].bitcast(I32),
             )
@@ -151,8 +144,8 @@ def tile_list_moromi_umami_features_kernel(
                 in_=w2_bf[a][:, t0:t1, :, :].rearrange("p t m j -> p (t m j)"),
             )
 
-        w1_codes = keep.tile([P, PASSES, PACK, 2 * P], U8, name="w1_codes", tag="after_z_a", align_bytes=64)
-        w1_sc = keep.tile([P, PASSES, PACK, P], U8, name="w1_sc", tag="after_z_b", align_bytes=64)
+        w1_codes = reuse.tile([P, PASSES, PACK, 2 * P], U8, name="w1_codes", offset=0, align_bytes=64)
+        w1_sc = reuse.tile([P, PASSES, PACK, P], U8, name="w1_sc", offset=18432, align_bytes=64)
         nc.vector.tensor_copy(
             out=w1_codes[:].bitcast(U16),
             in_=w1_raw[:].bitcast(U16).rearrange("p a (m t) -> p a t m", t=PACK),
@@ -173,6 +166,27 @@ def tile_list_moromi_umami_features_kernel(
         quantize_w2(2, 0, 1)
         quantize_w2(2, 1, 2)
         quantize_w2(2, 2, 4)
+
+        pages = [keep.tile([P, T2], F32, name="page%d" % t) for t in range(PACK)]
+        wgs_second = keep.tile([P, 1, S], F32, name="wgs_second")
+        wgs_rest = keep.tile([P, 2, S], F32, name="wgs_rest")
+        wgs_sb = [wgs_first[:, 0, :], wgs_second[:, 0, :], wgs_rest[:, 0, :], wgs_rest[:, 1, :]]
+        w3_raw = reuse.tile([P, PACK, N], F32, name="w3_raw", offset=12288, align_bytes=64)
+        nc.sync.dma_start(out=pages[0][:], in_=page_rows[:, 0, :])
+        nc.sync.dma_start(idx3[:], offs3)
+        nc.sync.dma_start(out=mu_sb[:], in_=mu.rearrange("(p t) -> p t", t=PACK))
+        nc.sync.dma_start(out=w3_raw[:], in_=w3.rearrange("(p j) n -> p j n", j=PACK))
+        for q in (0, 2):
+            load_wgs(wgs_second, 1, 2, q)
+        nc.sync.dma_start(out=pages[1][:], in_=page_rows[:, 1, :])
+        for q in (1, 3):
+            load_wgs(wgs_second, 1, 2, q)
+        for q in (0, 2):
+            load_wgs(wgs_rest, 2, 4, q)
+        nc.sync.dma_start(out=pages[2][:], in_=page_rows[:, 2, :])
+        for q in (1, 3):
+            load_wgs(wgs_rest, 2, 4, q)
+        nc.sync.dma_start(out=pages[3][:], in_=page_rows[:, 3, :])
 
         w3_bf = keep.tile([P, N, PACK], BF16, name="w3_bf", align_bytes=64)
         w3_codes = keep.tile([P, N], U32, name="w3_codes", align_bytes=64)
@@ -251,16 +265,16 @@ def tile_list_moromi_umami_features_kernel(
                 bend(t, u)
         prepare_w3()
 
-        x_bf = keep.tile([P, R, PACK], BF16, name="x_bf", tag="after_z_b", align_bytes=64)
-        page_all = keep.tile([P, T2, PACK], BF16, name="page_bf", tag="after_z_a", align_bytes=64)
-        page_bf = [page_all[:, c * BANK : (c + 1) * BANK, :] for c in range(CHUNKS)]
+        x_bf = reuse.tile([P, R, PACK], BF16, name="x_bf", offset=16384, align_bytes=64)
+        page_all = reuse.tile([P, T2, PACK], BF16, name="page_bf", offset=0, align_bytes=64)
+        V0, V1 = 256, 1536
 
-        def round_page(engine_copy, t, c):
-            cols = pages[t][:, c * BANK : (c + 1) * BANK]
-            if t == PACK - 2 and c in (1, 2):
-                engine_copy(out=page_bf[c][:, :, t : t + 2], in_=cols.unsqueeze(2).to_broadcast([P, BANK, 2]))
+        def round_page(engine_copy, t, m0, m1):
+            cols = pages[t][:, m0:m1]
+            if t == PACK - 2 and m0 == V0:
+                engine_copy(out=page_all[:, m0:m1, t : t + 2], in_=cols.unsqueeze(2).to_broadcast([P, m1 - m0, 2]))
             else:
-                engine_copy(out=page_bf[c][:, :, t], in_=cols)
+                engine_copy(out=page_all[:, m0:m1, t], in_=cols)
 
         def pick_x(t):
             picked = keep.tile([P, R], F32, name="picked%d" % t)
@@ -269,49 +283,32 @@ def tile_list_moromi_umami_features_kernel(
 
         for t in range(PACK):
             if t > 0:
-                nc.vector.tensor_tensor(pages[t][:].indirect(idx2[:]), h[t][:], wgs_sb[t][:], ALU.mult)
-            store_queue = nc.gpsimd if t + 1 < PACK else nc.sync
-            store_queue.dma_start(out=out_1_rows[:, t, :], in_=pages[t][:])
+                nc.vector.tensor_tensor(pages[t][:].indirect(idx2[:]), h[t][:], wgs_sb[t], ALU.mult)
+            nc.sync.dma_start(out=out_1_rows[:, t, :], in_=pages[t][:])
             if t + 1 < PACK:
                 if t > 0:
                     for u in range(HALVES):
                         add_plain(t + 1, u)
                 pick_x(t)
-                for c in range(CHUNKS):
-                    round_page(nc.scalar.copy, t, c)
+                if t == PACK - 2:
+                    for m0, m1 in ((0, V0), (V0, V1), (V1, T2)):
+                        round_page(nc.scalar.copy, t, m0, m1)
+                else:
+                    round_page(nc.scalar.copy, t, 0, T2)
 
         last = PACK - 1
-        y_codes = [keep.tile([P, BANK], U32, name="y_codes%d" % c, align_bytes=64) for c in range(CHUNKS)]
-        y_sc = keep.tile([P, T2], U8, name="y_sc", align_bytes=64)
-        out_2_words = out_2[0].rearrange("p m i -> p (m i)").bitcast(I32)
-
-        def quantize_page(c):
-            nc.vector.quantize_mx(
-                out=y_codes[c][:].bitcast(FP8X4),
-                scales=y_sc[:, c * BANK : (c + 1) * BANK],
-                in_=page_bf[c].rearrange("p m t -> p (m t)"),
-            )
-            nc.sync.dma_start(out=out_2_words[:, c * BANK : (c + 1) * BANK], in_=y_codes[c][:].bitcast(I32))
-
-        round_page(nc.scalar.copy, last, 0)
+        round_page(nc.scalar.copy, last, 0, V0)
         pick_x(last)
-        round_page(nc.vector.tensor_copy, last, 1)
-        quantize_page(0)
-        round_page(nc.vector.tensor_copy, last, 2)
-        round_page(nc.scalar.copy, last, 3)
+        nc.vector.tensor_copy(out=page_all[:, V0:V1, last], in_=pages[last][:, V0:V1])
+        round_page(nc.scalar.copy, last, V1, T2)
 
         x_codes = keep.tile([P, R], U32, name="x_codes", align_bytes=64)
         x_sc = keep.tile([P, R], U8, name="x_sc", align_bytes=64)
         nc.vector.quantize_mx(
             out=x_codes[:].bitcast(FP8X4), scales=x_sc[:], in_=x_bf[:].rearrange("p m t -> p (m t)")
         )
-        for c in range(1, CHUNKS):
-            quantize_page(c)
-        for q in range(QUADS):
-            nc.sync.dma_start(
-                out=out_3[0, 4 * q : 4 * q + 4, :].bitcast(I32), in_=y_sc[32 * q : 32 * q + 4, :].bitcast(I32)
-            )
 
+        y = keep.tile([P, N // P, R], F32, name="y")
         for b in range(N // P):
             acc = psum.tile([P, R], F32, name="z")
             nc.tensor.matmul_mx(
@@ -323,9 +320,23 @@ def tile_list_moromi_umami_features_kernel(
                 start=True,
                 stop=True,
             )
-            y = keep.tile([P, R], F32, name="y%d" % b)
-            if b == 1:
-                nc.vector.tensor_copy(out=y[:], in_=acc[:])
-            else:
-                nc.scalar.copy(out=y[:], in_=acc[:])
-            nc.sync.dma_start(out=out_0[b * P : (b + 1) * P, :], in_=y[:])
+            nc.scalar.copy(out=y[:, b, :], in_=acc[:])
+        out_0_rows = out_0.rearrange("(b p) j -> p b j", p=P)
+        for b0, b1_ in ((0, 2), (2, 3)):
+            nc.scalar.dma_start(out=out_0_rows[:, b0:b1_, :], in_=y[:, b0:b1_, :])
+
+        page_codes = keep.tile([P, T2], U32, name="page_codes", align_bytes=64)
+        page_sc = reuse.tile([P, T2], U8, name="page_sc", offset=16384, align_bytes=64)
+        out_2_words = out_2[0].rearrange("p m i -> p (m i)").bitcast(I32)
+        for m0, m1 in ((0, 512), (512, 1536), (1536, T2)):
+            nc.vector.quantize_mx(
+                out=page_codes[:, m0:m1].bitcast(FP8X4),
+                scales=page_sc[:, m0:m1],
+                in_=page_all[:, m0:m1, :].rearrange("p m t -> p (m t)"),
+            )
+            nc.sync.dma_start(out=out_2_words[:, m0:m1], in_=page_codes[:, m0:m1].bitcast(I32))
+        for q in range(QUADS):
+            queue = nc.sync if q % 2 == 0 else nc.scalar
+            queue.dma_start(
+                out=out_3[0, 4 * q : 4 * q + 4, :].bitcast(I32), in_=page_sc[32 * q : 32 * q + 4, :].bitcast(I32)
+            )

@@ -24,6 +24,9 @@ BANK = 512
 HALVES = S // BANK
 CHUNKS = T2 // BANK
 MOVED_ROWS = 112
+Z_BANKS = ((0, 2), (6, 7), (1, 1), (3, 3))
+PLAIN_BANKS = ((1, 3), (4, 5), (0, 2), (6, 7))
+Y_BANKS = (1, 3, 4)
 
 
 def tile_list_moromi_umami_features_kernel(
@@ -36,7 +39,7 @@ def tile_list_moromi_umami_features_kernel(
         keep = ctx.enter_context(tc.tile_pool(name="keep", bufs=1))
         ring = ctx.enter_context(tc.tile_pool(name="ring", bufs=2))
         reuse = ctx.enter_context(tc.tile_pool(name="reuse", bufs=1))
-        psum = ctx.enter_context(tc.psum_pool(name="psum", bufs=4))
+        psum = ctx.enter_context(tc.psum_pool(name="psum", bufs=1))
 
         idx = lists.tile([P, S // 16], U16, name="idx")
         idx2 = lists.tile([P, S // 16], U16, name="idx2")
@@ -73,32 +76,29 @@ def tile_list_moromi_umami_features_kernel(
         def load_wgs(tile, t0, t1, q):
             nc.sync.dma_start(out=tile[32 * q : 32 * q + 32, :, :], in_=wgs_rows[:, t0:t1, :])
 
-        for sb, vec in ((b1_sb, b1), (gain_sb, gain)):
-            nc.scalar.dma_start(out=sb[:], in_=vec.rearrange("(p t) -> p t", t=PACK))
+        wgs_first = keep.tile([P, 1, S], F32, name="wgs_first")
+        load_tab(0)
         for q in range(QUADS):
-            nc.scalar.dma_start(
+            nc.sync.dma_start(
                 out=tab_sc[32 * q : 32 * q + 4 * PASSES, :].bitcast(I32),
                 in_=tab_scales[:, 4 * q : 4 * q + 4, :].bitcast(I32),
             )
+        nc.sync.dma_start(out=w1_raw[:].bitcast(I32), in_=w1_words.rearrange("a p c -> p a c").bitcast(I32))
+        nc.sync.dma_start(out=w2_raw[0][:], in_=w2_rows[0])
         for q in range(QUADS):
-            nc.scalar.dma_start(
+            nc.sync.dma_start(
                 out=w1_sc_raw[32 * q : 32 * q + 4, :, :].bitcast(I32),
                 in_=w1_scales[:, 4 * q : 4 * q + 4, :].rearrange("a r c -> r a c").bitcast(I32),
             )
-
-        wgs_first = keep.tile([P, 1, S], F32, name="wgs_first")
-        load_tab(0)
-        nc.sync.dma_start(out=w1_raw[:].bitcast(I32), in_=w1_words.rearrange("a p c -> p a c").bitcast(I32))
-        nc.sync.dma_start(out=w2_raw[0][:], in_=w2_rows[0])
-        load_wgs(wgs_first, 0, 1, 0)
         load_tab(1)
-        load_wgs(wgs_first, 0, 1, 2)
         nc.sync.dma_start(out=w2_raw[1][:], in_=w2_rows[1])
-        load_wgs(wgs_first, 0, 1, 1)
         load_tab(2)
-        load_wgs(wgs_first, 0, 1, 3)
         for u in range(2):
             nc.sync.dma_start(out=w2_last[u][:], in_=w2_rows[2][:, :, u * (H // 2) : (u + 1) * (H // 2)])
+        for sb, vec in ((b1_sb, b1), (gain_sb, gain)):
+            nc.sync.dma_start(out=sb[:], in_=vec.rearrange("(p t) -> p t", t=PACK))
+        for q in (0, 2, 1, 3):
+            load_wgs(wgs_first, 0, 1, q)
         nc.sync.dma_start(idx2[:], offs2)
 
         v_sc = keep.tile([P, S], U8, name="v_sc", align_bytes=64)
@@ -168,7 +168,7 @@ def tile_list_moromi_umami_features_kernel(
         quantize_w2(2, 2, 4)
 
         pages = [keep.tile([P, T2], F32, name="page%d" % t) for t in range(PACK)]
-        wgs_second = keep.tile([P, 1, S], F32, name="wgs_second")
+        wgs_second = keep.tile([P, 1, S], F32, name="wgs_second", tag="second", align_bytes=64)
         wgs_rest = keep.tile([P, 2, S], F32, name="wgs_rest")
         wgs_sb = [wgs_first[:, 0, :], wgs_second[:, 0, :], wgs_rest[:, 0, :], wgs_rest[:, 1, :]]
         w3_raw = reuse.tile([P, PACK, N], F32, name="w3_raw", offset=12288, align_bytes=64)
@@ -188,28 +188,12 @@ def tile_list_moromi_umami_features_kernel(
             load_wgs(wgs_rest, 2, 4, q)
         nc.sync.dma_start(out=pages[3][:], in_=page_rows[:, 3, :])
 
-        w3_bf = keep.tile([P, N, PACK], BF16, name="w3_bf", align_bytes=64)
-        w3_codes = keep.tile([P, N], U32, name="w3_codes", align_bytes=64)
-        w3_sc = keep.tile([P, N], U8, name="w3_sc", align_bytes=64)
-
-        def prepare_w3():
-            nc.scalar.copy(
-                out=w3_bf[:].rearrange("p (c i) j -> p c j i", i=4),
-                in_=w3_raw[:].rearrange("p j (c i) -> p c j i", i=4),
-            )
-            for n0, n1 in ((0, 256), (256, N)):
-                nc.vector.quantize_mx(
-                    out=w3_codes[:, n0:n1].bitcast(FP8X4),
-                    scales=w3_sc[:, n0:n1],
-                    in_=w3_bf[:, n0:n1, :].rearrange("p n j -> p (n j)"),
-                )
-
-        bent = [keep.tile([P, S], F32, name="bent%d" % t) for t in range(PACK)]
+        bent = [keep.tile([P, S], F32, name="bent%d" % t, tag="bent%d" % t, align_bytes=64) for t in range(PACK)]
         h = {}
 
         def bend(t, u):
             cols = slice(u * BANK, (u + 1) * BANK)
-            z = psum.tile([P, BANK], F32, name="z")
+            z = psum.tile([P, BANK], F32, name="z", tag="bank%d" % Z_BANKS[t][u])
             for a in range(PASSES):
                 nc.tensor.matmul_mx(
                     out=z[:],
@@ -226,7 +210,7 @@ def tile_list_moromi_umami_features_kernel(
             cols = slice(u * BANK, (u + 1) * BANK)
             if u == 0:
                 h[t] = ring.tile([P, S], F32, name="h")
-            plain = psum.tile([P, BANK], F32, name="plain")
+            plain = psum.tile([P, BANK], F32, name="plain", tag="bank%d" % PLAIN_BANKS[t][u])
             for a in range(PASSES):
                 nc.tensor.matmul_mx(
                     out=plain[:],
@@ -263,7 +247,11 @@ def tile_list_moromi_umami_features_kernel(
         for t in range(2, PACK):
             for u in range(HALVES):
                 bend(t, u)
-        prepare_w3()
+        w3_bf = keep.tile([P, N, PACK], BF16, name="w3_bf", tag="bent0", align_bytes=64)
+        nc.scalar.copy(
+            out=w3_bf[:].rearrange("p (c i) j -> p c j i", i=4),
+            in_=w3_raw[:].rearrange("p j (c i) -> p c j i", i=4),
+        )
 
         x_bf = reuse.tile([P, R, PACK], BF16, name="x_bf", offset=16384, align_bytes=64)
         page_all = reuse.tile([P, T2, PACK], BF16, name="page_bf", offset=0, align_bytes=64)
@@ -296,6 +284,15 @@ def tile_list_moromi_umami_features_kernel(
                 else:
                     round_page(nc.scalar.copy, t, 0, T2)
 
+        w3_codes = keep.tile([P, N], U32, name="w3_codes", tag="second", align_bytes=64)
+        w3_sc = keep.tile([P, N], U8, name="w3_sc", align_bytes=64)
+        for n0, n1 in ((0, 256), (256, N)):
+            nc.vector.quantize_mx(
+                out=w3_codes[:, n0:n1].bitcast(FP8X4),
+                scales=w3_sc[:, n0:n1],
+                in_=w3_bf[:, n0:n1, :].rearrange("p n j -> p (n j)"),
+            )
+
         last = PACK - 1
         round_page(nc.scalar.copy, last, 0, V0)
         pick_x(last)
@@ -310,7 +307,7 @@ def tile_list_moromi_umami_features_kernel(
 
         y = keep.tile([P, N // P, R], F32, name="y")
         for b in range(N // P):
-            acc = psum.tile([P, R], F32, name="z")
+            acc = psum.tile([P, R], F32, name="acc", tag="bank%d" % Y_BANKS[b])
             nc.tensor.matmul_mx(
                 out=acc[:],
                 lhsT=w3_codes[:, b * P : (b + 1) * P].bitcast(FP8X4),

from contextlib import ExitStack

import concourse.mybir as mybir

K, H, N, T, S, T2, R = 1536, 512, 384, 2048, 1024, 2048, 512
FLOPS = 2 * (2 * K * H * S + H * N * R)

F32 = mybir.dt.float32
BF16 = mybir.dt.bfloat16
I32 = mybir.dt.int32
U32 = mybir.dt.uint32
U16 = mybir.dt.uint16
U8 = mybir.dt.uint8
FP8X4 = mybir.dt.float8_e4m3fn_x4
FP4X4 = mybir.dt.float4_e2m1fn_x4
ACT = mybir.ActivationFunctionType
ALU = mybir.AluOpType

P = 128
PACK = 4
PASSES = K // (P * PACK)
QUADS = 4
BANK = 512
HALVES = S // BANK
CHUNKS = T2 // BANK
MOVED_ROWS = 112
Z_BANKS = ((0, 2), (6, 7), (1, 1), (3, 3))
PLAIN_BANKS = ((1, 3), (4, 5), (0, 2), (6, 7))
Y_BANKS = (1, 3, 4)


def tile_list_moromi_umami_features_kernel(
    tc, tab_words, tab_scales, offs, offs2, offs3, w1_words, w1_scales, b1, gain, w2, wgs, page0, mu, w3,
    out_0, out_1, out_2, out_3,
):
    nc = tc.nc
    with ExitStack() as ctx:
        lists = ctx.enter_context(tc.tile_pool(name="lists", bufs=1))
        keep = ctx.enter_context(tc.tile_pool(name="keep", bufs=1))
        ring = ctx.enter_context(tc.tile_pool(name="ring", bufs=2))
        reuse = ctx.enter_context(tc.tile_pool(name="reuse", bufs=1))
        psum = ctx.enter_context(tc.psum_pool(name="psum", bufs=1))

        idx = lists.tile([P, S // 16], U16, name="idx")
        idx2 = lists.tile([P, S // 16], U16, name="idx2")
        idx3 = lists.tile([P, R // 16], U16, name="idx3")

        tab_sc = keep.tile([P, T], U8, name="tab_sc", align_bytes=64)
        nc.vector.memset(tab_sc[:].bitcast(I32), 0)
        w1_sc_raw = keep.tile([P, PASSES, H], U8, name="w1_sc_raw", align_bytes=64)
        nc.vector.memset(w1_sc_raw[:].rearrange("p a c -> p (a c)").bitcast(I32), 0)
        v_sc_moved = [keep.tile([P, S], U8, name="v_sc_moved%d" % a, align_bytes=64) for a in range(1, PASSES)]
        for moved in v_sc_moved:
            nc.vector.memset(moved[:].bitcast(I32), 0)
        warm = keep.tile([P, 8], F32, name="warm")
        nc.vector.memset(warm[:, 0:4], 0.0)
        nc.scalar.activation(out=warm[:, 4:5], in_=warm[:, 0:1], func=ACT.Tanh)

        nc.sync.dma_start(idx[:], offs)
        b1_sb = keep.tile([P, PACK], F32, name="b1_sb")
        gain_sb = keep.tile([P, PACK], F32, name="gain_sb")
        mu_sb = keep.tile([P, PACK], F32, name="mu_sb")

        tab_w = [keep.tile([P, T], I32, name="tab_w%d" % a) for a in range(PASSES)]
        w1_raw = keep.tile([P, PASSES, 2 * H], U8, name="w1_raw")
        w2_raw = [keep.tile([P, PACK, H], F32, name="w2_raw%d" % a) for a in range(PASSES - 1)]
        w2_last = [keep.tile([P, PACK, H // 2], F32, name="w2_last%d" % u) for u in range(2)]
        w2_rows = w2.rearrange("(a p j) c -> a p j c", p=P, j=PACK)
        wgs_rows = wgs.rearrange("(i t) s -> i t s", t=PACK)
        page_rows = page0.rearrange("(p t) m -> p t m", t=PACK)
        out_1_rows = out_1.rearrange("(p t) m -> p t m", t=PACK)

        def load_tab(a):
            nc.sync.dma_start(out=tab_w[a][:], in_=tab_words[a].rearrange("p t i -> p (t i)").bitcast(I32))

        def load_wgs(tile, t0, t1, q):
            nc.sync.dma_start(out=tile[32 * q : 32 * q + 32, :, :], in_=wgs_rows[:, t0:t1, :])

        wgs_first = keep.tile([P, 1, S], F32, name="wgs_first")
        load_tab(0)
        for q in range(QUADS):
            nc.sync.dma_start(
                out=tab_sc[32 * q : 32 * q + 4 * PASSES, :].bitcast(I32),
                in_=tab_scales[:, 4 * q : 4 * q + 4, :].bitcast(I32),
            )
        nc.sync.dma_start(out=w1_raw[:].bitcast(I32), in_=w1_words.rearrange("a p c -> p a c").bitcast(I32))
        nc.sync.dma_start(out=w2_raw[0][:], in_=w2_rows[0])
        for q in range(QUADS):
            nc.sync.dma_start(
                out=w1_sc_raw[32 * q : 32 * q + 4, :, :].bitcast(I32),
                in_=w1_scales[:, 4 * q : 4 * q + 4, :].rearrange("a r c -> r a c").bitcast(I32),
            )
        load_tab(1)
        nc.sync.dma_start(out=w2_raw[1][:], in_=w2_rows[1])
        load_tab(2)
        for u in range(2):
            nc.sync.dma_start(out=w2_last[u][:], in_=w2_rows[2][:, :, u * (H // 2) : (u + 1) * (H // 2)])
        for sb, vec in ((b1_sb, b1), (gain_sb, gain)):
            nc.sync.dma_start(out=sb[:], in_=vec.rearrange("(p t) -> p t", t=PACK))
        for q in (0, 2, 1, 3):
            load_wgs(wgs_first, 0, 1, q)
        nc.sync.dma_start(idx2[:], offs2)

        v_sc = keep.tile([P, S], U8, name="v_sc", align_bytes=64)
        nc.vector.tensor_copy(out=v_sc[:], in_=tab_sc[:].indirect(idx[:]))
        for a in range(1, PASSES):
            nc.scalar.dma_start(
                out=v_sc_moved[a - 1][0:MOVED_ROWS, :].bitcast(I32),
                in_=v_sc[4 * a : 4 * a + MOVED_ROWS, :].bitcast(I32),
            )
        v_sc_zero = [v_sc] + v_sc_moved

        v_w = [[None] * HALVES for a in range(PASSES)]

        def gather_words(a, whole):
            if whole:
                both = keep.tile([P, S], U32, name="v_w%d" % a, align_bytes=64)
                nc.vector.tensor_copy(out=both[:], in_=tab_w[a][:].bitcast(U32).indirect(idx[:]))
                for u in range(HALVES):
                    v_w[a][u] = both[:, u * BANK : (u + 1) * BANK]
            else:
                for u in range(HALVES):
                    half = keep.tile([P, BANK], U32, name="v_w%d_%d" % (a, u), align_bytes=64)
                    nc.vector.tensor_copy(
                        out=half[:],
                        in_=tab_w[a][:].bitcast(U32).indirect(idx[:, u * (BANK // 16) : (u + 1) * (BANK // 16)]),
                    )
                    v_w[a][u] = half[:]

        w2_bf = [keep.tile([P, PACK, P, PACK], BF16, name="w2_bf%d" % a, align_bytes=64) for a in range(PASSES)]
        w2_codes = [keep.tile([P, H], U32, name="w2_codes%d" % a, align_bytes=64) for a in range(PASSES)]
        w2_sc = [keep.tile([P, H], U8, name="w2_sc%d" % a, align_bytes=64) for a in range(PASSES)]

        def deal_w2(engine_copy, a, raw, m0, m1):
            engine_copy(
                out=w2_bf[a][:, :, m0:m1, :].rearrange("p t m j -> p m t j"),
                in_=raw[:].rearrange("p j (m t) -> p m t j", t=PACK),
            )

        def quantize_w2(a, t0, t1):
            nc.vector.quantize_mx(
                out=w2_codes[a][:, t0 * P : t1 * P].bitcast(FP8X4),
                scales=w2_sc[a][:, t0 * P : t1 * P],
                in_=w2_bf[a][:, t0:t1, :, :].rearrange("p t m j -> p (t m j)"),
            )

        w1_codes = reuse.tile([P, PASSES, PACK, 2 * P], U8, name="w1_codes", offset=0, align_bytes=64)
        w1_sc = reuse.tile([P, PASSES, PACK, P], U8, name="w1_sc", offset=18432, align_bytes=64)
        nc.vector.tensor_copy(
            out=w1_codes[:].bitcast(U16),
            in_=w1_raw[:].bitcast(U16).rearrange("p a (m t) -> p a t m", t=PACK),
        )
        gather_words(0, True)
        nc.vector.tensor_copy(
            out=w1_sc[:],
            in_=w1_sc_raw[:].rearrange("p a (m t) -> p a t m", t=PACK),
        )
        deal_w2(nc.scalar.copy, 0, w2_raw[0], 0, P)
        gather_words(1, True)
        quantize_w2(0, 0, PACK)
        deal_w2(nc.scalar.copy, 1, w2_raw[1], 0, P)
        gather_words(2, False)
        quantize_w2(1, 0, PACK)
        deal_w2(nc.scalar.copy, 2, w2_last[0], 0, P // 2)
        deal_w2(nc.vector.tensor_copy, 2, w2_last[1], P // 2, P)
        quantize_w2(2, 0, 1)
        quantize_w2(2, 1, 2)
        quantize_w2(2, 2, 4)

        pages = [keep.tile([P, T2], F32, name="page%d" % t) for t in range(PACK)]
        wgs_second = keep.tile([P, 1, S], F32, name="wgs_second", tag="second", align_bytes=64)
        wgs_rest = keep.tile([P, 2, S], F32, name="wgs_rest")
        wgs_sb = [wgs_first[:, 0, :], wgs_second[:, 0, :], wgs_rest[:, 0, :], wgs_rest[:, 1, :]]
        w3_raw = reuse.tile([P, PACK, N], F32, name="w3_raw", offset=12288, align_bytes=64)
        nc.sync.dma_start(out=pages[0][:], in_=page_rows[:, 0, :])
        nc.sync.dma_start(idx3[:], offs3)
        nc.sync.dma_start(out=mu_sb[:], in_=mu.rearrange("(p t) -> p t", t=PACK))
        nc.sync.dma_start(out=w3_raw[:], in_=w3.rearrange("(p j) n -> p j n", j=PACK))
        for q in (0, 2):
            load_wgs(wgs_second, 1, 2, q)
        nc.sync.dma_start(out=pages[1][:], in_=page_rows[:, 1, :])
        for q in (1, 3):
            load_wgs(wgs_second, 1, 2, q)
        for q in (0, 2):
            load_wgs(wgs_rest, 2, 4, q)
        nc.sync.dma_start(out=pages[2][:], in_=page_rows[:, 2, :])
        for q in (1, 3):
            load_wgs(wgs_rest, 2, 4, q)
        nc.sync.dma_start(out=pages[3][:], in_=page_rows[:, 3, :])

        bent = [keep.tile([P, S], F32, name="bent%d" % t, tag="bent%d" % t, align_bytes=64) for t in range(PACK)]
        h = {}

        def bend(t, u):
            cols = slice(u * BANK, (u + 1) * BANK)
            z = psum.tile([P, BANK], F32, name="z", tag="bank%d" % Z_BANKS[t][u])
            for a in range(PASSES):
                nc.tensor.matmul_mx(
                    out=z[:],
                    lhsT=w1_codes[:, a, t, :].bitcast(FP4X4),
                    lhsT_scale=w1_sc[:, a, t, :],
                    rhs=v_w[a][u].bitcast(FP8X4),
                    rhs_scale=v_sc_zero[a][:, cols],
                    start=(a == 0),
                    stop=(a == PASSES - 1),
                )
            nc.scalar.activation(out=bent[t][:, cols], in_=z[:], func=ACT.Tanh, bias=b1_sb[:, t : t + 1])

        def add_plain(t, u):
            cols = slice(u * BANK, (u + 1) * BANK)
            if u == 0:
                h[t] = ring.tile([P, S], F32, name="h")
            plain = psum.tile([P, BANK], F32, name="plain", tag="bank%d" % PLAIN_BANKS[t][u])
            for a in range(PASSES):
                nc.tensor.matmul_mx(
                    out=plain[:],
                    lhsT=w2_codes[a][:, t * P : (t + 1) * P].bitcast(FP8X4),
                    lhsT_scale=w2_sc[a][:, t * P : (t + 1) * P],
                    rhs=v_w[a][u].bitcast(FP8X4),
                    rhs_scale=v_sc[4 * a : P, cols],
                    start=(a == 0),
                    stop=(a == PASSES - 1),
                )
            nc.vector.scalar_tensor_tensor(
                out=h[t][:, cols],
                in0=bent[t][:, cols],
                scalar=gain_sb[:, t : t + 1],
                in1=plain[:],
                op0=ALU.mult,
                op1=ALU.add,
            )

        for u in range(HALVES):
            cols = slice(u * BANK, (u + 1) * BANK)
            bend(0, u)
            add_plain(0, u)
            nc.vector.tensor_tensor(
                pages[0][:].indirect(idx2[:, u * (BANK // 16) : (u + 1) * (BANK // 16)]),
                h[0][:, cols],
                wgs_sb[0][:, cols],
                ALU.mult,
            )
        for u in range(HALVES):
            bend(1, u)
        for u in range(HALVES):
            add_plain(1, u)
        for t in range(2, PACK):
            for u in range(HALVES):
                bend(t, u)
        w3_bf = keep.tile([P, N, PACK], BF16, name="w3_bf", tag="bent0", align_bytes=64)
        nc.scalar.copy(
            out=w3_bf[:].rearrange("p (c i) j -> p c j i", i=4),
            in_=w3_raw[:].rearrange("p j (c i) -> p c j i", i=4),
        )

        x_bf = reuse.tile([P, R, PACK], BF16, name="x_bf", offset=16384, align_bytes=64)
        page_all = reuse.tile([P, T2, PACK], BF16, name="page_bf", offset=0, align_bytes=64)
        V0, V1 = 256, 1536

        def round_page(engine_copy, t, m0, m1):
            cols = pages[t][:, m0:m1]
            if t == PACK - 2 and m0 == V0:
                engine_copy(out=page_all[:, m0:m1, t : t + 2], in_=cols.unsqueeze(2).to_broadcast([P, m1 - m0, 2]))
            else:
                engine_copy(out=page_all[:, m0:m1, t], in_=cols)

        def pick_x(t):
            picked = keep.tile([P, R], F32, name="picked%d" % t)
            nc.vector.tensor_copy(out=picked[:], in_=pages[t][:].indirect(idx3[:]))
            nc.scalar.activation(out=x_bf[:, :, t], in_=picked[:], func=ACT.Abs, bias=mu_sb[:, t : t + 1], scale=-1.0)

        for t in range(PACK):
            if t > 0:
                nc.vector.tensor_tensor(pages[t][:].indirect(idx2[:]), h[t][:], wgs_sb[t], ALU.mult)
            nc.sync.dma_start(out=out_1_rows[:, t, :], in_=pages[t][:])
            if t + 1 < PACK:
                if t > 0:
                    for u in range(HALVES):
                        add_plain(t + 1, u)
                pick_x(t)
                if t == PACK - 2:
                    for m0, m1 in ((0, V0), (V0, V1), (V1, T2)):
                        round_page(nc.scalar.copy, t, m0, m1)
                else:
                    round_page(nc.scalar.copy, t, 0, T2)

        w3_codes = keep.tile([P, N], U32, name="w3_codes", tag="second", align_bytes=64)
        w3_sc = keep.tile([P, N], U8, name="w3_sc", align_bytes=64)
        for n0, n1 in ((0, 256), (256, N)):
            nc.vector.quantize_mx(
                out=w3_codes[:, n0:n1].bitcast(FP8X4),
                scales=w3_sc[:, n0:n1],
                in_=w3_bf[:, n0:n1, :].rearrange("p n j -> p (n j)"),
            )

        last = PACK - 1
        round_page(nc.scalar.copy, last, 0, V0)
        pick_x(last)
        nc.vector.tensor_copy(out=page_all[:, V0:V1, last], in_=pages[last][:, V0:V1])
        round_page(nc.scalar.copy, last, V1, T2)

        x_codes = keep.tile([P, R], U32, name="x_codes", align_bytes=64)
        x_sc = keep.tile([P, R], U8, name="x_sc", align_bytes=64)
        nc.vector.quantize_mx(
            out=x_codes[:].bitcast(FP8X4), scales=x_sc[:], in_=x_bf[:].rearrange("p m t -> p (m t)")
        )

        y = keep.tile([P, N // P, R], F32, name="y")
        for b in range(N // P):
            acc = psum.tile([P, R], F32, name="acc", tag="bank%d" % Y_BANKS[b])
            nc.tensor.matmul_mx(
                out=acc[:],
                lhsT=w3_codes[:, b * P : (b + 1) * P].bitcast(FP8X4),
                lhsT_scale=w3_sc[:, b * P : (b + 1) * P],
                rhs=x_codes[:].bitcast(FP8X4),
                rhs_scale=x_sc[:],
                start=True,
                stop=True,
            )
            nc.scalar.copy(out=y[:, b, :], in_=acc[:])
        out_0_rows = out_0.rearrange("(b p) j -> p b j", p=P)
        for b0, b1_ in ((0, 2), (2, 3)):
            nc.scalar.dma_start(out=out_0_rows[:, b0:b1_, :], in_=y[:, b0:b1_, :])

        page_codes = keep.tile([P, T2], U32, name="page_codes", align_bytes=64)
        page_sc = reuse.tile([P, T2], U8, name="page_sc", offset=16384, align_bytes=64)
        out_2_words = out_2[0].rearrange("p m i -> p (m i)").bitcast(I32)
        for m0, m1 in ((0, 512), (512, 1536), (1536, T2)):
            nc.vector.quantize_mx(
                out=page_codes[:, m0:m1].bitcast(FP8X4),
                scales=page_sc[:, m0:m1],
                in_=page_all[:, m0:m1, :].rearrange("p m t -> p (m t)"),
            )
            nc.sync.dma_start(out=out_2_words[:, m0:m1], in_=page_codes[:, m0:m1].bitcast(I32))
        for q in range(QUADS):
            queue = nc.sync if q % 2 == 0 else nc.scalar
            queue.dma_start(
                out=out_3[0, 4 * q : 4 * q + 4, :].bitcast(I32), in_=page_sc[32 * q : 32 * q + 4, :].bitcast(I32)
            )
